import numpy as np
import ml_dtypes


def mxq(x, axis, fmt="e4m3"):
    dtype, down = {"e4m3": (ml_dtypes.float8_e4m3fn, 7), "e5m2": (ml_dtypes.float8_e5m2, 14)}[fmt]
    v = np.moveaxis(np.asarray(x, np.float32).astype(ml_dtypes.bfloat16).astype(np.float64), axis, -1)
    blocks = v.reshape(v.shape[:-1] + (-1, 32))
    amax = np.abs(blocks).max(-1, keepdims=True)
    byte = np.maximum(np.where(amax > 0, np.frexp(amax)[1] - 1 + 127, 0) - down, 1)
    scale = np.exp2(byte - 127.0)
    codes = (blocks / scale).astype(np.float32).astype(dtype).astype(np.float64)
    return np.moveaxis((codes * scale).reshape(v.shape), -1, axis)


WIDE = False


def mx_kscale(k):
    if not WIDE:
        return np.ones(k)
    levels = np.array([10, -10, 5, -5, 0])
    if k % 512:
        return np.exp2(np.random.permutation(np.resize(levels, k // 32))).repeat(32)
    a = np.empty((k // 512, 16))
    for p in range(k // 512):
        a[p, :8] = np.random.permutation(np.resize(levels, 8))
        for g in range(8):
            far = levels[np.abs(levels - a[p, g]) >= 10]
            a[p, g + 8] = far[np.random.randint(len(far))]
    return np.exp2(a.ravel()).repeat(32)


def f64(x):
    return np.asarray(x).astype(np.float64)


def striped(idx):
    return np.tile(idx.reshape(-1, 16).T, (8, 1)).astype(np.uint16)


def unstriped(offs):
    return offs[:16].T.reshape(-1).astype(np.int64)


E2M1 = np.array([0.0, 0.5, 1.0, 1.5, 2.0, 3.0, 4.0, 6.0, -0.0, -0.5, -1.0, -1.5, -2.0, -3.0, -4.0, -6.0])


def pack_weight(w, fmt):
    k, n = w.shape
    w = f64(np.asarray(w, np.float32).astype(ml_dtypes.bfloat16)).reshape(k // 32, 32, n)
    amax = np.abs(w).max(1)
    if fmt == "e4m3":
        byte = np.frexp(amax)[1] - 1 + 127 - 7
    else:
        mant, ex = np.frexp(amax / 6.0)
        byte = np.where(mant > 0.5, ex, ex - 1) + 127
    byte = np.clip(np.where(amax > 0, byte, 1), 1, 254)
    scaled = (w * np.exp2(127.0 - byte)[:, None, :]).reshape(k, n).astype(np.float32)
    by_word = np.ascontiguousarray(scaled.reshape(k // 512, 128, 4, n).transpose(0, 1, 3, 2))
    if fmt == "e4m3":
        words = by_word.astype(ml_dtypes.float8_e4m3fn).view(np.uint8)
    else:
        c = by_word.astype(ml_dtypes.float4_e2m1fn).view(np.uint8) & 0xF
        words = (c[..., 0::2] | (c[..., 1::2] << 4)).reshape(k // 512, 128, 2 * n)
    return np.ascontiguousarray(words), np.ascontiguousarray(byte.astype(np.uint8).reshape(k // 512, 16, n))


def unpack_weight(words, scales, fmt):
    g, _, n = scales.shape
    words = np.ascontiguousarray(words).reshape(g, 128, n, -1)
    if fmt == "e4m3":
        vals = words.view(ml_dtypes.float8_e4m3fn).astype(np.float64)
    else:
        nib = np.empty((g, 128, n, 4), np.uint8)
        nib[..., 0::2] = words & 0xF
        nib[..., 1::2] = words >> 4
        vals = E2M1[nib]
    vals = vals * np.repeat(np.exp2(scales.astype(np.float64) - 127.0), 8, axis=1)[..., None]
    return vals.transpose(0, 1, 3, 2).reshape(g * 512, n)


def gelu(v):
    return 0.5 * v * (1.0 + np.tanh(np.sqrt(2.0 / np.pi) * (v + 0.044715 * v**3)))


K, H, T, S, T2, P = 512, 1024, 4096, 1024, 2048, 1024

def setup_inputs():
    n = np.random.standard_normal
    s = mx_kscale(K)[:, None]
    u = mx_kscale(H)[:, None]
    tab_words, tab_scales = pack_weight(n((K, T)) * s, "e4m3")
    w2_words, w2_scales = pack_weight(n((K, H)) / np.sqrt(K) / s * u.T, "e2m1")
    return {
        "tab_words": tab_words, "tab_scales": tab_scales,
        "offs": striped(np.random.permutation(T)[:S]),
        "offs2": striped(np.random.permutation(T2)[:S]),
        "offs3": striped(np.random.permutation(T2)[:P]),
        "offs4": striped(np.random.permutation(T2)[:P]),
        "w1": (n((K, H)) / np.sqrt(K) / s * u.T).astype(np.float32),
        "w2_words": w2_words, "w2_scales": w2_scales,
        "shift": (0.8 * n((H, S)) * u).astype(np.float32),
        "page0": (n((H, T2)) * u).astype(np.float32),
        "wgs": np.exp(0.3 * n((128, S))).astype(np.float32),
        "lim": (0.6 * n(H) * u[:, 0]).astype(np.float32),
        "load": np.exp(0.5 * n((H, P))).astype(np.float32),
        "w3": (n((H, H)) / np.sqrt(H) / u * u.T).astype(np.float32),
        "base": (0.6 * n(H) * u[:, 0]).astype(np.float32),
        "wgo": np.exp(0.3 * n((128, P))).astype(np.float32),
    }

def reference(tab_words, tab_scales, offs, offs2, offs3, offs4, w1, w2_words, w2_scales,
              shift, page0, wgs, lim, load, w3, base, wgo):
    v = unpack_weight(tab_words, tab_scales, "e4m3")[:, unstriped(offs)]
    w2 = unpack_weight(w2_words, w2_scales, "e2m1")
    a1 = mxq(f64(w1), 0, "e4m3").T @ v
    a2 = w2.T @ v
    h = np.maximum(a1, a2 + f64(shift))
    page = f64(page0).copy()
    page[:, unstriped(offs2)] = np.tile(f64(wgs), (H // 128, 1)) * h
    x = np.maximum(page[:, unstriped(offs3)], f64(lim)[:, None]) * f64(load)
    d = mxq(f64(w3), 0, "e4m3").T @ mxq(x, 0, "e4m3")
    y = np.maximum(d, f64(base)[:, None]) + x
    page[:, unstriped(offs4)] = np.tile(f64(wgo), (H // 128, 1)) * y
    return page

@@ -1,0 +1,318 @@
+from contextlib import ExitStack
+
+import concourse.mybir as mybir
+from concourse.masks import make_identity
+
+K, H, T, S, T2, NP = 512, 1024, 4096, 1024, 2048, 1024
+FLOPS = 2 * (2 * K * H * S + H * H * NP)
+
+F32 = mybir.dt.float32
+BF16 = mybir.dt.bfloat16
+I32 = mybir.dt.int32
+U32 = mybir.dt.uint32
+U16 = mybir.dt.uint16
+U8 = mybir.dt.uint8
+FP8X4 = mybir.dt.float8_e4m3fn_x4
+FP4X4 = mybir.dt.float4_e2m1fn_x4
+ALU = mybir.AluOpType
+ACT = mybir.ActivationFunctionType
+
+P = 128
+PACK = 4
+HALF = 512
+BLOCKS = HALF // P
+SLICES = H // P
+LIST_HALF = HALF // 16
+FIRST_DEFERRED = 4
+LAG = 4
+
+
+def tile_list_electrode_heat_page_kernel(
+    tc, tab_words, tab_scales, offs, offs2, offs3, offs4, w1, w2_words, w2_scales,
+    shift, page0, wgs, lim, load, w3, base, wgo, out,
+):
+    nc = tc.nc
+
+    def rows(dram, s):
+        return dram.rearrange("(a p t) c -> a t p c", p=P, t=PACK)[s // PACK, s % PACK]
+
+    def cols(hf):
+        return slice(hf * HALF, (hf + 1) * HALF)
+
+    def entries(hf):
+        return slice(hf * LIST_HALF, (hf + 1) * LIST_HALF)
+
+    def block(b):
+        return slice(b * P, (b + 1) * P)
+
+    with ExitStack() as ctx:
+        lists = ctx.enter_context(tc.tile_pool(name="lists", bufs=1))
+        keep = ctx.enter_context(tc.tile_pool(name="keep", bufs=1))
+        ring = ctx.enter_context(tc.tile_pool(name="ring", bufs=2))
+        psum = ctx.enter_context(tc.psum_pool(name="psum", bufs=1))
+
+        def load_list(dram, name):
+            tile = lists.tile([P, S // 16], U16, name=name)
+            nc.sync.dma_start(tile[:], dram)
+            return tile
+
+        def load_vector(dram, name):
+            tile = keep.tile([P, SLICES], F32, name=name)
+            nc.sync.dma_start(
+                tile[:].rearrange("p (a t) -> p a t", t=PACK), dram.rearrange("(a p t) -> p a t", p=P, t=PACK)
+            )
+            return tile
+
+        def load_scale_rows(queue, tile, dram):
+            for q in range(4):
+                queue.dma_start(tile[32 * q : 32 * q + 4, :].bitcast(I32), dram[0, 4 * q : 4 * q + 4, :].bitcast(I32))
+
+        def load_dealt(tile, dram, t0, t1):
+            by_row = dram.rearrange("(q t) j -> q t j", t=PACK)
+            for c in range(4):
+                nc.sync.dma_start(tile[32 * c : 32 * (c + 1), :, :], by_row[:, t0:t1, :])
+
+        w2_s_raw = keep.tile([P, H], U8, name="w2_s_raw", align_bytes=64)
+        nc.vector.memset(w2_s_raw[:].bitcast(I32), 0)
+        tab_s = keep.tile([P, T], U8, name="tab_s", align_bytes=64)
+        nc.vector.memset(tab_s[:].bitcast(I32), 0)
+
+        idx = load_list(offs, "idx")
+        w2_w_raw = keep.tile([P, 2 * H], U8, name="w2_w_raw", align_bytes=64)
+        nc.sync.dma_start(w2_w_raw[:].bitcast(I32), w2_words[0].bitcast(I32))
+        idx2 = load_list(offs2, "idx2")
+        load_scale_rows(nc.sync, w2_s_raw, w2_scales)
+        tab_w = keep.tile([P, T], U32, name="tab_w", tag="table", align_bytes=64)
+        nc.sync.dma_start(tab_w[:].bitcast(I32), tab_words[0].rearrange("p t i -> p (t i)").bitcast(I32))
+        load_scale_rows(nc.sync, tab_s, tab_scales)
+
+        def load_weight(dram, a, n_half, slot):
+            raw = keep.tile([P, PACK, HALF], F32, name="raw", tag="page%d" % slot)
+            k_rows = dram[a * P * PACK : (a + 1) * P * PACK, cols(n_half)]
+            nc.sync.dma_start(raw[:], k_rows.rearrange("(p j) c -> p j c", j=PACK))
+            return raw
+
+        def quantise(grouped, name, tag):
+            codes = keep.tile([P, HALF], U32, name=name + "_c", tag=tag, align_bytes=64)
+            scales = keep.tile([P, HALF], U8, name=name + "_s", align_bytes=64)
+            nc.vector.quantize_mx(out=codes[:].bitcast(FP8X4), scales=scales[:], in_=grouped[:])
+            return codes, scales
+
+        def quantise_weight(raw, name):
+            grouped = ring.tile([P, PACK * HALF], BF16, name="grouped", align_bytes=64)
+            dst = grouped[:].rearrange("p (t m j) -> p m j t", t=PACK, j=PACK)
+            src = raw[:].rearrange("p j (m t) -> p m j t", t=PACK)
+            for m0 in range(0, P, P // 2):
+                nc.scalar.copy(dst[:, m0 : m0 + P // 2], src[:, m0 : m0 + P // 2])
+            return quantise(grouped, name, name)
+
+        def quantise_x(x_tile, name, tag):
+            grouped = ring.tile([P, PACK * HALF], BF16, name="grouped", align_bytes=64)
+            nc.scalar.copy(
+                grouped[:].rearrange("p (c i t) -> p c t i", i=4, t=PACK),
+                x_tile[:].rearrange("p t (c i) -> p c t i", i=4),
+            )
+            return quantise(grouped, name, tag)
+
+        def load_page(s):
+            tile = keep.tile([P, T2], F32, name="page", tag="page%d" % s)
+            nc.sync.dma_start(tile[:], rows(page0, s))
+            return tile
+
+        def load_half(dram, s, hf, name):
+            tile = ring.tile([P, HALF], F32, name=name, bufs=6)
+            nc.sync.dma_start(tile[:], rows(dram, s)[:, cols(hf)])
+            return tile
+
+        def load_wgs(t):
+            tile = keep.tile([P, 1, S], F32, name="wgs%d" % t)
+            load_dealt(tile, wgs, t, t + 1)
+            return tile
+
+        w1_raw = [load_weight(w1, 0, 0, 2)]
+        pages = [load_page(0)]
+        shifts = {(0, 0): load_half(shift, 0, 0, "shift_t")}
+        wgs_t = [load_wgs(0)]
+        shifts[(0, 1)] = load_half(shift, 0, 1, "shift_t")
+        idx3 = load_list(offs3, "idx3")
+        lim_t = load_vector(lim, "lim_t")
+        idx4 = load_list(offs4, "idx4")
+        base_t = load_vector(base, "base_t")
+
+        ident = keep.tile([P, P], F32, name="ident")
+        make_identity(nc, ident[:])
+        neg_base = keep.tile([P, SLICES], F32, name="neg_base")
+        nc.scalar.activation(neg_base[:], base_t[:], ACT.Copy, scale=-1.0)
+
+        w2_w = keep.tile([P, 2 * H], U8, name="w2_w", align_bytes=64)
+        nc.vector.tensor_copy(
+            w2_w[:].rearrange("p (a t m b) -> p a t m b", a=2, t=PACK, b=2),
+            w2_w_raw[:].rearrange("p (a m t b) -> p a t m b", a=2, t=PACK, b=2),
+        )
+        w2_s = keep.tile([P, H], U8, name="w2_s", align_bytes=64)
+        nc.vector.tensor_copy(
+            w2_s[:].rearrange("p (a t m) -> p a t m", a=2, t=PACK),
+            w2_s_raw[:].rearrange("p (a m t) -> p a t m", a=2, t=PACK),
+        )
+        v_w, v_s = [], []
+        for hf in range(2):
+            words = keep.tile([P, HALF], U32, name="v_w%d" % hf, align_bytes=64)
+            nc.vector.tensor_copy(words[:], tab_w[:].indirect(idx[:, entries(hf)]))
+            scale_bytes = keep.tile([P, HALF], U8, name="v_s%d" % hf, align_bytes=64)
+            nc.vector.tensor_copy(scale_bytes[:], tab_s[:].indirect(idx[:, entries(hf)]))
+            v_w.append(words)
+            v_s.append(scale_bytes)
+        w1_q = [quantise_weight(w1_raw[0], "w1_0")]
+
+        def bank(tag, bufs):
+            return psum.tile([P, HALF], F32, name=tag, tag=tag, bufs=bufs)
+
+        def add_transposed(dst, terms):
+            for b in range(BLOCKS):
+                for i, term in enumerate(terms):
+                    nc.tensor.matmul(
+                        dst[:, block(b)], term[:, block(b)], ident[:],
+                        start=(i == 0), stop=(i == len(terms) - 1), is_transpose=True,
+                    )
+
+        def staged(name):
+            return ring.tile([P, HALF], F32, name=name, tag=name)
+
+        def first_products(s, hf):
+            a, t = s // PACK, s % PACK
+            a2 = bank("mx", 3)
+            nc.tensor.matmul_mx(
+                out=a2[:], lhsT=w2_w[:, 2 * s * P : 2 * (s + 1) * P].bitcast(FP4X4), lhsT_scale=w2_s[:, block(s)],
+                rhs=v_w[hf][:].bitcast(FP8X4), rhs_scale=v_s[hf][:], start=True, stop=True,
+            )
+            a1 = bank("mx", 3)
+            nc.tensor.matmul_mx(
+                out=a1[:], lhsT=w1_q[a][0][:, block(t)].bitcast(FP8X4), lhsT_scale=w1_q[a][1][:, block(t)],
+                rhs=v_w[hf][:].bitcast(FP8X4), rhs_scale=v_s[hf][:], start=True, stop=True,
+            )
+            return a1, a2
+
+        def make_h(s):
+            h = ring.tile([P, S], F32, name="h", tag="result", bufs=3)
+            for hf in range(2):
+                a1, a2 = first_products(s, hf)
+                shift_t = shifts.pop((s, hf))
+                if s == 0:
+                    b = staged("st_a")
+                    nc.vector.tensor_tensor(b[:], a2[:], shift_t[:], ALU.add)
+                    nc.vector.tensor_tensor(h[:, cols(hf)], a1[:], b[:], ALU.max)
+                else:
+                    a2_sb = staged("st_a")
+                    nc.scalar.copy(a2_sb[:], a2[:])
+                    neg_a1 = staged("st_b")
+                    nc.scalar.activation(neg_a1[:], a1[:], ACT.Copy, scale=-1.0)
+                    excess = bank("turned", 3)
+                    add_transposed(excess, [shift_t, a2_sb, neg_a1])
+                    neg_a1_turned = bank("turned", 3)
+                    add_transposed(neg_a1_turned, [neg_a1])
+                    relu_turned = staged("st_c")
+                    nc.scalar.activation(relu_turned[:], excess[:], ACT.Relu)
+                    a1_turned = staged("st_d")
+                    nc.scalar.activation(a1_turned[:], neg_a1_turned[:], ACT.Copy, scale=-1.0)
+                    total = bank("back", 2)
+                    add_transposed(total, [relu_turned, a1_turned])
+                    nc.scalar.copy(h[:, cols(hf)], total[:])
+            return h
+
+        x = [[keep.tile([P, PACK, HALF], F32, name="x%d%d" % (a, hf)) for hf in range(2)] for a in range(2)]
+        loads = {}
+
+        def pick(s, hf):
+            picked = staged("picked")
+            nc.vector.tensor_copy(picked[:], pages[s][:].indirect(idx3[:, entries(hf)]))
+            return picked
+
+        def prepare(s, hf, picked):
+            nc.vector.scalar_tensor_tensor(
+                out=x[s // PACK][hf][:, s % PACK, :], in0=picked[:], scalar=lim_t[:, s : s + 1],
+                in1=loads.pop((s, hf))[:], op0=ALU.max, op1=ALU.mult,
+            )
+
+        x_q = {}
+        w3_q = {}
+        wgo_t = None
+        h_next = make_h(0)
+        for s in range(SLICES):
+            halves = [0, 1] if s < FIRST_DEFERRED else [0]
+            h = h_next
+            if s + 1 < SLICES:
+                for hf in range(2):
+                    shifts[(s + 1, hf)] = load_half(shift, s + 1, hf, "shift_t")
+                if s + 1 < PACK:
+                    wgs_t.append(load_wgs(s + 1))
+                pages.append(load_page(s + 1))
+            for hf in halves:
+                loads[(s, hf)] = load_half(load, s, hf, "load_t")
+            if s == 0:
+                w1_raw.append(load_weight(w1, 0, 1, 3))
+            if s + 1 < SLICES:
+                h_next = make_h(s + 1)
+
+            weights = wgs_t[s % PACK]
+            if s == 0:
+                for hf in range(2):
+                    nc.vector.tensor_tensor(
+                        pages[s][:].indirect(idx2[:, entries(hf)]), h[:, cols(hf)], weights[:, 0, cols(hf)], ALU.mult
+                    )
+            else:
+                nc.vector.tensor_tensor(pages[s][:].indirect(idx2[:]), h[:], weights[:, 0, :], ALU.mult)
+            picked = [pick(s, hf) for hf in halves]
+            for hf in halves:
+                prepare(s, hf, picked[hf])
+
+            if s == 0:
+                w1_q.append(quantise_weight(w1_raw[1], "w1_1"))
+            if s < 4:
+                key = (s % 2, s // 2)
+                w3_q[key] = quantise_weight(load_weight(w3, key[0], key[1], 4 + s), "w3_%d" % s)
+            if s == 2:
+                wgo_t = keep.tile([P, PACK, NP], F32, name="wgo_t", tag="table", align_bytes=64)
+                load_dealt(wgo_t, wgo, 0, PACK)
+            if s == PACK - 1:
+                for hf in range(2):
+                    x_q[(0, hf)] = quantise_x(x[0][hf], "xq0%d" % hf, "xq0%d" % hf)
+        x_q[(1, 0)] = quantise_x(x[1][0], "xq10", "xq10")
+        for s in range(FIRST_DEFERRED, SLICES):
+            loads[(s, 1)] = load_half(load, s, 1, "load_t")
+            prepare(s, 1, pick(s, 1))
+
+        def score(s, hf, direct):
+            a, t = s // PACK, s % PACK
+            d = bank("mx", 3)
+            for g in range(2):
+                nc.tensor.matmul_mx(
+                    out=d[:], lhsT=w3_q[(g, a)][0][:, block(t)].bitcast(FP8X4), lhsT_scale=w3_q[(g, a)][1][:, block(t)],
+                    rhs=x_q[(g, hf)][0][:].bitcast(FP8X4), rhs_scale=x_q[(g, hf)][1][:], start=(g == 0), stop=(g == 1),
+                )
+            x_rows = x[a][hf][:, t, :]
+            if direct:
+                y = keep.tile([P, HALF], F32, name="y_first", tag="xq11", align_bytes=64)
+                nc.vector.scalar_tensor_tensor(
+                    out=y[:], in0=d[:], scalar=base_t[:, s : s + 1], in1=x_rows, op0=ALU.max, op1=ALU.add
+                )
+            else:
+                above = staged("st_a")
+                nc.scalar.activation(above[:], d[:], ACT.Relu, bias=neg_base[:, s : s + 1])
+                turned = bank("turned", 3)
+                add_transposed(turned, [x_rows, above])
+                turned_sb = staged("st_c")
+                nc.scalar.copy(turned_sb[:], turned[:])
+                total = bank("back", 2)
+                add_transposed(total, [turned_sb])
+                y = ring.tile([P, HALF], F32, name="y", tag="result", bufs=3)
+                nc.scalar.activation(y[:], total[:], ACT.Identity, bias=base_t[:, s : s + 1])
+            nc.vector.tensor_tensor(pages[s][:].indirect(idx4[:, entries(hf)]), y[:], wgo_t[:, t, cols(hf)], ALU.mult)
+
+        for step in range(SLICES + LAG):
+            if step < SLICES:
+                score(step, 0, step == 0)
+            if step == 0:
+                x_q[(1, 1)] = quantise_x(x[1][1], "xq11", "xq11")
+            if step >= LAG:
+                score(step - LAG, 1, False)
+                nc.sync.dma_start(rows(out, step - LAG), pages[step - LAG][:])

@@ -25,6 +25,8 @@ SLICES = H // P
 LIST_HALF = HALF // 16
 FIRST_DEFERRED = 4
 LAG = 4
+DIRECT_EVERY = 4
+DIRECT_EVERY_Y = 4
 
 
 def tile_list_electrode_heat_page_kernel(
@@ -69,7 +71,7 @@ def tile_list_electrode_heat_page_kernel(
 
         def load_dealt(tile, dram, t0, t1):
             by_row = dram.rearrange("(q t) j -> q t j", t=PACK)
-            for c in range(4):
+            for c in (0, 2, 1, 3):
                 nc.sync.dma_start(tile[32 * c : 32 * (c + 1), :, :], by_row[:, t0:t1, :])
 
         w2_s_raw = keep.tile([P, H], U8, name="w2_s_raw", align_bytes=64)
@@ -86,9 +88,9 @@ def tile_list_electrode_heat_page_kernel(
         nc.sync.dma_start(tab_w[:].bitcast(I32), tab_words[0].rearrange("p t i -> p (t i)").bitcast(I32))
         load_scale_rows(nc.sync, tab_s, tab_scales)
 
-        def load_weight(dram, a, n_half, slot):
-            raw = keep.tile([P, PACK, HALF], F32, name="raw", tag="page%d" % slot)
-            k_rows = dram[a * P * PACK : (a + 1) * P * PACK, cols(n_half)]
+        def load_weight(dram, g, c0, width, slot):
+            raw = keep.tile([P, PACK, width], F32, name="raw", tag=slot)
+            k_rows = dram[g * P * PACK : (g + 1) * P * PACK, c0 : c0 + width]
             nc.sync.dma_start(raw[:], k_rows.rearrange("(p j) c -> p j c", j=PACK))
             return raw
 
@@ -98,16 +100,18 @@ def tile_list_electrode_heat_page_kernel(
             nc.vector.quantize_mx(out=codes[:].bitcast(FP8X4), scales=scales[:], in_=grouped[:])
             return codes, scales
 
-        def quantise_weight(raw, name):
-            grouped = ring.tile([P, PACK * HALF], BF16, name="grouped", align_bytes=64)
+        def quantise_weight(pieces, name, stage="grouped"):
+            grouped = ring.tile([P, PACK * HALF], BF16, name="grouped", tag=stage, align_bytes=64)
             dst = grouped[:].rearrange("p (t m j) -> p m j t", t=PACK, j=PACK)
-            src = raw[:].rearrange("p j (m t) -> p m j t", t=PACK)
-            for m0 in range(0, P, P // 2):
-                nc.scalar.copy(dst[:, m0 : m0 + P // 2], src[:, m0 : m0 + P // 2])
+            for i, piece in enumerate(pieces):
+                nc.scalar.copy(dst[:, i * P // 2 : (i + 1) * P // 2], piece.rearrange("p j (m t) -> p m j t", t=PACK))
             return quantise(grouped, name, name)
 
-        def quantise_x(x_tile, name, tag):
-            grouped = ring.tile([P, PACK * HALF], BF16, name="grouped", align_bytes=64)
+        def both_halves(raw):
+            return [raw[:, :, 0 : HALF // 2], raw[:, :, HALF // 2 : HALF]]
+
+        def quantise_x(x_tile, name, tag, stage="grouped"):
+            grouped = ring.tile([P, PACK * HALF], BF16, name="grouped", tag=stage, align_bytes=64)
             nc.scalar.copy(
                 grouped[:].rearrange("p (c i t) -> p c t i", i=4, t=PACK),
                 x_tile[:].rearrange("p t (c i) -> p c t i", i=4),
@@ -125,11 +129,11 @@ def tile_list_electrode_heat_page_kernel(
             return tile
 
         def load_wgs(t):
-            tile = keep.tile([P, 1, S], F32, name="wgs%d" % t)
+            tile = keep.tile([P, 1, S], F32, name="wgs%d" % t, tag="wgs%d" % t)
             load_dealt(tile, wgs, t, t + 1)
             return tile
 
-        w1_raw = [load_weight(w1, 0, 0, 2)]
+        w1_raw = [load_weight(w1, 0, 0, HALF, "page2")]
         pages = [load_page(0)]
         shifts = {(0, 0): load_half(shift, 0, 0, "shift_t")}
         wgs_t = [load_wgs(0)]
@@ -162,7 +166,7 @@ def tile_list_electrode_heat_page_kernel(
             nc.vector.tensor_copy(scale_bytes[:], tab_s[:].indirect(idx[:, entries(hf)]))
             v_w.append(words)
             v_s.append(scale_bytes)
-        w1_q = [quantise_weight(w1_raw[0], "w1_0")]
+        w1_q = [quantise_weight(both_halves(w1_raw[0]), "w1_0")]
 
         def bank(tag, bufs):
             return psum.tile([P, HALF], F32, name=tag, tag=tag, bufs=bufs)
@@ -176,48 +180,70 @@ def tile_list_electrode_heat_page_kernel(
                     )
 
         def staged(name):
-            return ring.tile([P, HALF], F32, name=name, tag=name)
+            return ring.tile([P, HALF], F32, name=name, tag=name, align_bytes=64)
 
-        def first_products(s, hf):
+        def first_products(s, hf, banks):
             a, t = s // PACK, s % PACK
-            a2 = bank("mx", 3)
+            a2 = bank(banks, 2)
             nc.tensor.matmul_mx(
                 out=a2[:], lhsT=w2_w[:, 2 * s * P : 2 * (s + 1) * P].bitcast(FP4X4), lhsT_scale=w2_s[:, block(s)],
                 rhs=v_w[hf][:].bitcast(FP8X4), rhs_scale=v_s[hf][:], start=True, stop=True,
             )
-            a1 = bank("mx", 3)
+            a1 = bank(banks, 2)
             nc.tensor.matmul_mx(
                 out=a1[:], lhsT=w1_q[a][0][:, block(t)].bitcast(FP8X4), lhsT_scale=w1_q[a][1][:, block(t)],
                 rhs=v_w[hf][:].bitcast(FP8X4), rhs_scale=v_s[hf][:], start=True, stop=True,
             )
             return a1, a2
 
-        def make_h(s):
-            h = ring.tile([P, S], F32, name="h", tag="result", bufs=3)
-            for hf in range(2):
-                a1, a2 = first_products(s, hf)
-                shift_t = shifts.pop((s, hf))
-                if s == 0:
-                    b = staged("st_a")
-                    nc.vector.tensor_tensor(b[:], a2[:], shift_t[:], ALU.add)
-                    nc.vector.tensor_tensor(h[:, cols(hf)], a1[:], b[:], ALU.max)
-                else:
-                    a2_sb = staged("st_a")
-                    nc.scalar.copy(a2_sb[:], a2[:])
-                    neg_a1 = staged("st_b")
-                    nc.scalar.activation(neg_a1[:], a1[:], ACT.Copy, scale=-1.0)
-                    excess = bank("turned", 3)
-                    add_transposed(excess, [shift_t, a2_sb, neg_a1])
-                    neg_a1_turned = bank("turned", 3)
-                    add_transposed(neg_a1_turned, [neg_a1])
-                    relu_turned = staged("st_c")
-                    nc.scalar.activation(relu_turned[:], excess[:], ACT.Relu)
-                    a1_turned = staged("st_d")
-                    nc.scalar.activation(a1_turned[:], neg_a1_turned[:], ACT.Copy, scale=-1.0)
-                    total = bank("back", 2)
-                    add_transposed(total, [relu_turned, a1_turned])
-                    nc.scalar.copy(h[:, cols(hf)], total[:])
-            return h
+        h_tiles = {}
+        under_way = {}
+
+        def on_vector(u):
+            return u < 2 or u % DIRECT_EVERY == 2
+
+        def h_products(u):
+            s, hf = u // 2, u % 2
+            if hf == 0:
+                h_tiles[s] = ring.tile([P, S], F32, name="h", tag="result", bufs=3)
+            shift_t = shifts.pop((s, hf))
+            if on_vector(u):
+                a1, a2 = first_products(s, hf, "mx" if u == 1 else "direct")
+                shifted = staged("picked")
+                nc.vector.tensor_tensor(shifted[:], a2[:], shift_t[:], ALU.add)
+                nc.vector.tensor_tensor(h_tiles[s][:, cols(hf)], a1[:], shifted[:], ALU.max)
+            else:
+                a1, a2 = first_products(s, hf, "mx")
+                a2_sb = staged("st_a")
+                nc.scalar.copy(a2_sb[:], a2[:])
+                neg_a1 = staged("st_b")
+                nc.scalar.activation(neg_a1[:], a1[:], ACT.Copy, scale=-1.0)
+                under_way[u] = (shift_t, a2_sb, neg_a1)
+
+        def h_excess(u):
+            if u in under_way:
+                shift_t, a2_sb, neg_a1 = under_way[u]
+                excess = bank("turned", 2)
+                add_transposed(excess, [shift_t, a2_sb, neg_a1])
+                neg_a1_turned = bank("turned", 2)
+                add_transposed(neg_a1_turned, [neg_a1])
+                relu_turned = staged("st_c")
+                nc.scalar.activation(relu_turned[:], excess[:], ACT.Relu)
+                a1_turned = staged("st_d")
+                nc.scalar.activation(a1_turned[:], neg_a1_turned[:], ACT.Copy, scale=-1.0)
+                under_way[u] = (relu_turned, a1_turned)
+
+        def h_finish(u):
+            if u in under_way:
+                total = bank("back", 2)
+                add_transposed(total, under_way.pop(u))
+                nc.scalar.copy(h_tiles[u // 2][:, cols(u % 2)], total[:])
+
+        def h_step(u):
+            if u < 2 * SLICES:
+                h_products(u)
+            h_excess(u - 1)
+            h_finish(u - 2)
 
         x = [[keep.tile([P, PACK, HALF], F32, name="x%d%d" % (a, hf)) for hf in range(2)] for a in range(2)]
         loads = {}
@@ -233,26 +259,31 @@ def tile_list_electrode_heat_page_kernel(
                 in1=loads.pop((s, hf))[:], op0=ALU.max, op1=ALU.mult,
             )
 
+        def load_slice(s):
+            for hf in range(2):
+                shifts[(s, hf)] = load_half(shift, s, hf, "shift_t")
+
         x_q = {}
         w3_q = {}
+        w3_late = []
         wgo_t = None
-        h_next = make_h(0)
+        load_slice(1)
+        for u in range(4):
+            h_step(u)
         for s in range(SLICES):
             halves = [0, 1] if s < FIRST_DEFERRED else [0]
-            h = h_next
             if s + 1 < SLICES:
-                for hf in range(2):
-                    shifts[(s + 1, hf)] = load_half(shift, s + 1, hf, "shift_t")
                 if s + 1 < PACK:
                     wgs_t.append(load_wgs(s + 1))
                 pages.append(load_page(s + 1))
+            if s + 2 < SLICES:
+                load_slice(s + 2)
             for hf in halves:
                 loads[(s, hf)] = load_half(load, s, hf, "load_t")
             if s == 0:
-                w1_raw.append(load_weight(w1, 0, 1, 3))
-            if s + 1 < SLICES:
-                h_next = make_h(s + 1)
+                w1_raw.append(load_weight(w1, 0, HALF, HALF, "page3"))
 
+            h = h_tiles.pop(s)
             weights = wgs_t[s % PACK]
             if s == 0:
                 for hf in range(2):
@@ -264,55 +295,93 @@ def tile_list_electrode_heat_page_kernel(
             picked = [pick(s, hf) for hf in halves]
             for hf in halves:
                 prepare(s, hf, picked[hf])
+            if s + 1 < SLICES:
+                for u in (2 * s + 4, 2 * s + 5):
+                    h_step(u)
 
             if s == 0:
-                w1_q.append(quantise_weight(w1_raw[1], "w1_1"))
-            if s < 4:
-                key = (s % 2, s // 2)
-                w3_q[key] = quantise_weight(load_weight(w3, key[0], key[1], 4 + s), "w3_%d" % s)
-            if s == 2:
+                w1_q.append(quantise_weight(both_halves(w1_raw[1]), "w1_1"))
+            if s in (1, 2):
+                raw = load_weight(w3, s - 1, 0, HALF, "page%d" % (s + 3))
+                w3_q[(s - 1, 0)] = quantise_weight(both_halves(raw), "w3_%d0" % (s - 1))
+            if s == 4:
                 wgo_t = keep.tile([P, PACK, NP], F32, name="wgo_t", tag="table", align_bytes=64)
                 load_dealt(wgo_t, wgo, 0, PACK)
-            if s == PACK - 1:
-                for hf in range(2):
-                    x_q[(0, hf)] = quantise_x(x[0][hf], "xq0%d" % hf, "xq0%d" % hf)
+            if s >= PACK:
+                i = s - PACK
+                w3_late.append(load_weight(w3, i // 2, HALF + (i % 2) * HALF // 2, HALF // 2, "wgs%d" % i))
+        for hf in range(2):
+            x_q[(0, hf)] = quantise_x(x[0][hf], "xq0%d" % hf, "xq0%d" % hf, "st_d")
         x_q[(1, 0)] = quantise_x(x[1][0], "xq10", "xq10")
         for s in range(FIRST_DEFERRED, SLICES):
             loads[(s, 1)] = load_half(load, s, 1, "load_t")
             prepare(s, 1, pick(s, 1))
 
-        def score(s, hf, direct):
+        order = []
+        for step in range(SLICES + LAG):
+            if step < SLICES:
+                order.append((step, 0))
+            if step >= LAG:
+                order.append((step - LAG, 1))
+        scored = {}
+
+        def y_product(i):
+            s, hf = order[i]
             a, t = s // PACK, s % PACK
-            d = bank("mx", 3)
+            direct = i % DIRECT_EVERY_Y == 0
+            d = bank("direct" if direct else "mx", 2)
             for g in range(2):
                 nc.tensor.matmul_mx(
                     out=d[:], lhsT=w3_q[(g, a)][0][:, block(t)].bitcast(FP8X4), lhsT_scale=w3_q[(g, a)][1][:, block(t)],
                     rhs=x_q[(g, hf)][0][:].bitcast(FP8X4), rhs_scale=x_q[(g, hf)][1][:], start=(g == 0), stop=(g == 1),
                 )
-            x_rows = x[a][hf][:, t, :]
             if direct:
-                y = keep.tile([P, HALF], F32, name="y_first", tag="xq11", align_bytes=64)
-                nc.vector.scalar_tensor_tensor(
-                    out=y[:], in0=d[:], scalar=base_t[:, s : s + 1], in1=x_rows, op0=ALU.max, op1=ALU.add
-                )
+                scored[i] = (True, d)
             else:
                 above = staged("st_a")
                 nc.scalar.activation(above[:], d[:], ACT.Relu, bias=neg_base[:, s : s + 1])
-                turned = bank("turned", 3)
-                add_transposed(turned, [x_rows, above])
+                scored[i] = (False, above)
+
+        def y_sum(i):
+            s, hf = order[i]
+            direct, above = scored[i]
+            if not direct:
+                turned = bank("turned", 2)
+                add_transposed(turned, [x[s // PACK][hf][:, s % PACK, :], above])
                 turned_sb = staged("st_c")
                 nc.scalar.copy(turned_sb[:], turned[:])
-                total = bank("back", 2)
-                add_transposed(total, [turned_sb])
-                y = ring.tile([P, HALF], F32, name="y", tag="result", bufs=3)
-                nc.scalar.activation(y[:], total[:], ACT.Identity, bias=base_t[:, s : s + 1])
-            nc.vector.tensor_tensor(pages[s][:].indirect(idx4[:, entries(hf)]), y[:], wgo_t[:, t, cols(hf)], ALU.mult)
+                scored[i] = (False, turned_sb)
 
-        for step in range(SLICES + LAG):
-            if step < SLICES:
-                score(step, 0, step == 0)
-            if step == 0:
+        def y_put(i):
+            s, hf = order[i]
+            direct, source = scored.pop(i)
+            if i == 0:
+                y = keep.tile([P, HALF], F32, name="y_first", tag="xq11", align_bytes=64)
+            else:
+                y = ring.tile([P, HALF], F32, name="y", tag="result", bufs=3)
+            if direct:
+                nc.vector.scalar_tensor_tensor(
+                    out=y[:], in0=source[:], scalar=base_t[:, s : s + 1], in1=x[s // PACK][hf][:, s % PACK, :],
+                    op0=ALU.max, op1=ALU.add,
+                )
+            else:
+                total = bank("back", 2)
+                add_transposed(total, [source])
+                nc.scalar.activation(y[:], total[:], ACT.Identity, bias=base_t[:, s : s + 1])
+            nc.vector.tensor_tensor(
+                pages[s][:].indirect(idx4[:, entries(hf)]), y[:], wgo_t[:, s % PACK, cols(hf)], ALU.mult
+            )
+            if hf == 1:
+                nc.sync.dma_start(rows(out, s), pages[s][:])
+
+        for i in range(len(order) + 2):
+            if i < len(order):
+                y_product(i)
+            if 1 <= i <= len(order):
+                y_sum(i - 1)
+            if i >= 2:
+                y_put(i - 2)
+            if i == 2:
                 x_q[(1, 1)] = quantise_x(x[1][1], "xq11", "xq11")
-            if step >= LAG:
-                score(step - LAG, 1, False)
-                nc.sync.dma_start(rows(out, step - LAG), pages[step - LAG][:])
+                for g in range(2):
+                    w3_q[(g, 1)] = quantise_weight([w3_late[2 * g][:], w3_late[2 * g + 1][:]], "w3_%d1" % g, "st_d")

@@ -69,9 +69,9 @@ def tile_list_electrode_heat_page_kernel(
             for q in range(4):
                 queue.dma_start(tile[32 * q : 32 * q + 4, :].bitcast(I32), dram[0, 4 * q : 4 * q + 4, :].bitcast(I32))
 
-        def load_dealt(tile, dram, t0, t1):
+        def load_dealt(tile, dram, t0, t1, quadrants):
             by_row = dram.rearrange("(q t) j -> q t j", t=PACK)
-            for c in (0, 2, 1, 3):
+            for c in quadrants:
                 nc.sync.dma_start(tile[32 * c : 32 * (c + 1), :, :], by_row[:, t0:t1, :])
 
         w2_s_raw = keep.tile([P, H], U8, name="w2_s_raw", align_bytes=64)
@@ -123,23 +123,31 @@ def tile_list_electrode_heat_page_kernel(
             nc.sync.dma_start(tile[:], rows(page0, s))
             return tile
 
-        def load_half(dram, s, hf, name):
-            tile = ring.tile([P, HALF], F32, name=name, bufs=6)
-            nc.sync.dma_start(tile[:], rows(dram, s)[:, cols(hf)])
+        def load_rows(dram, s, name, bufs):
+            tile = ring.tile([P, S], F32, name=name, bufs=bufs)
+            nc.sync.dma_start(tile[:], rows(dram, s))
             return tile
 
-        def load_wgs(t):
-            tile = keep.tile([P, 1, S], F32, name="wgs%d" % t, tag="wgs%d" % t)
-            load_dealt(tile, wgs, t, t + 1)
-            return tile
+        wgs_first = keep.tile([P, 1, S], F32, name="wgs_first")
+        wgs_second = keep.tile([P, 1, S], F32, name="wgs_second")
+        wgs_rest = keep.tile([P, 2, S], F32, name="wgs_rest")
+        wgs_t = [wgs_first[:, 0, :], wgs_second[:, 0, :], wgs_rest[:, 0, :], wgs_rest[:, 1, :]]
 
         w1_raw = [load_weight(w1, 0, 0, HALF, "page2")]
+        shifts = {0: load_rows(shift, 0, "shift_t", 3)}
+        load_dealt(wgs_first, wgs, 0, 1, (0, 2))
         pages = [load_page(0)]
-        shifts = {(0, 0): load_half(shift, 0, 0, "shift_t")}
-        wgs_t = [load_wgs(0)]
-        shifts[(0, 1)] = load_half(shift, 0, 1, "shift_t")
+        load_dealt(wgs_first, wgs, 0, 1, (1, 3))
+        shifts[1] = load_rows(shift, 1, "shift_t", 3)
+        loads = {0: load_rows(load, 0, "load_t", 4)}
         idx3 = load_list(offs3, "idx3")
         lim_t = load_vector(lim, "lim_t")
+        load_dealt(wgs_second, wgs, 1, 2, (0, 2))
+        pages.append(load_page(1))
+        load_dealt(wgs_second, wgs, 1, 2, (1, 3))
+        shifts[2] = load_rows(shift, 2, "shift_t", 3)
+        w1_raw.append(load_weight(w1, 0, HALF, HALF, "page3"))
+        load_dealt(wgs_rest, wgs, 2, 4, (0, 2, 1, 3))
         idx4 = load_list(offs4, "idx4")
         base_t = load_vector(base, "base_t")
 
@@ -166,7 +174,18 @@ def tile_list_electrode_heat_page_kernel(
             nc.vector.tensor_copy(scale_bytes[:], tab_s[:].indirect(idx[:, entries(hf)]))
             v_w.append(words)
             v_s.append(scale_bytes)
-        w1_q = [quantise_weight(both_halves(w1_raw[0]), "w1_0")]
+        grouped = ring.tile([P, PACK * HALF], BF16, name="grouped", tag="grouped", align_bytes=64)
+        w1_codes = keep.tile([P, HALF], U32, name="w1_0_c", align_bytes=64)
+        w1_scales = keep.tile([P, HALF], U8, name="w1_0_s", align_bytes=64)
+        dst = grouped[:].rearrange("p (t m j) -> p m j t", t=PACK, j=PACK)
+        src = w1_raw[0][:].rearrange("p j (m t) -> p m j t", t=PACK)
+        for t0, t1 in ((0, 1), (1, PACK)):
+            nc.scalar.copy(dst[:, :, :, t0:t1], src[:, :, :, t0:t1])
+            nc.vector.quantize_mx(
+                out=w1_codes[:, t0 * P : t1 * P].bitcast(FP8X4), scales=w1_scales[:, t0 * P : t1 * P],
+                in_=grouped[:, t0 * HALF : t1 * HALF],
+            )
+        w1_q = [(w1_codes, w1_scales)]
 
         def bank(tag, bufs):
             return psum.tile([P, HALF], F32, name=tag, tag=tag, bufs=bufs)
@@ -206,11 +225,11 @@ def tile_list_electrode_heat_page_kernel(
             s, hf = u // 2, u % 2
             if hf == 0:
                 h_tiles[s] = ring.tile([P, S], F32, name="h", tag="result", bufs=3)
-            shift_t = shifts.pop((s, hf))
+            shift_t = shifts[s][:, cols(hf)]
             if on_vector(u):
                 a1, a2 = first_products(s, hf, "mx" if u == 1 else "direct")
                 shifted = staged("picked")
-                nc.vector.tensor_tensor(shifted[:], a2[:], shift_t[:], ALU.add)
+                nc.vector.tensor_tensor(shifted[:], a2[:], shift_t, ALU.add)
                 nc.vector.tensor_tensor(h_tiles[s][:, cols(hf)], a1[:], shifted[:], ALU.max)
             else:
                 a1, a2 = first_products(s, hf, "mx")
@@ -229,7 +248,7 @@ def tile_list_electrode_heat_page_kernel(
                 add_transposed(neg_a1_turned, [neg_a1])
                 relu_turned = staged("st_c")
                 nc.scalar.activation(relu_turned[:], excess[:], ACT.Relu)
-                a1_turned = staged("st_d")
+                a1_turned = staged("grouped" if u // 2 == SLICES - 2 else "st_d")
                 nc.scalar.activation(a1_turned[:], neg_a1_turned[:], ACT.Copy, scale=-1.0)
                 under_way[u] = (relu_turned, a1_turned)
 
@@ -246,7 +265,6 @@ def tile_list_electrode_heat_page_kernel(
             h_finish(u - 2)
 
         x = [[keep.tile([P, PACK, HALF], F32, name="x%d%d" % (a, hf)) for hf in range(2)] for a in range(2)]
-        loads = {}
 
         def pick(s, hf):
             picked = staged("picked")
@@ -256,42 +274,32 @@ def tile_list_electrode_heat_page_kernel(
         def prepare(s, hf, picked):
             nc.vector.scalar_tensor_tensor(
                 out=x[s // PACK][hf][:, s % PACK, :], in0=picked[:], scalar=lim_t[:, s : s + 1],
-                in1=loads.pop((s, hf))[:], op0=ALU.max, op1=ALU.mult,
+                in1=loads[s][:, cols(hf)], op0=ALU.max, op1=ALU.mult,
             )
-
-        def load_slice(s):
-            for hf in range(2):
-                shifts[(s, hf)] = load_half(shift, s, hf, "shift_t")
 
         x_q = {}
         w3_q = {}
-        w3_late = []
         wgo_t = None
-        load_slice(1)
         for u in range(4):
             h_step(u)
         for s in range(SLICES):
             halves = [0, 1] if s < FIRST_DEFERRED else [0]
-            if s + 1 < SLICES:
-                if s + 1 < PACK:
-                    wgs_t.append(load_wgs(s + 1))
+            if 1 <= s < SLICES - 1:
                 pages.append(load_page(s + 1))
-            if s + 2 < SLICES:
-                load_slice(s + 2)
-            for hf in halves:
-                loads[(s, hf)] = load_half(load, s, hf, "load_t")
-            if s == 0:
-                w1_raw.append(load_weight(w1, 0, HALF, HALF, "page3"))
+            if 1 <= s < SLICES - 2:
+                shifts[s + 2] = load_rows(shift, s + 2, "shift_t", 3)
+            if s + 1 < SLICES:
+                loads[s + 1] = load_rows(load, s + 1, "load_t", 4)
 
             h = h_tiles.pop(s)
             weights = wgs_t[s % PACK]
             if s == 0:
                 for hf in range(2):
                     nc.vector.tensor_tensor(
-                        pages[s][:].indirect(idx2[:, entries(hf)]), h[:, cols(hf)], weights[:, 0, cols(hf)], ALU.mult
+                        pages[s][:].indirect(idx2[:, entries(hf)]), h[:, cols(hf)], weights[:, cols(hf)], ALU.mult
                     )
             else:
-                nc.vector.tensor_tensor(pages[s][:].indirect(idx2[:]), h[:], weights[:, 0, :], ALU.mult)
+                nc.vector.tensor_tensor(pages[s][:].indirect(idx2[:]), h[:], weights, ALU.mult)
             picked = [pick(s, hf) for hf in halves]
             for hf in halves:
                 prepare(s, hf, picked[hf])
@@ -301,20 +309,17 @@ def tile_list_electrode_heat_page_kernel(
 
             if s == 0:
                 w1_q.append(quantise_weight(both_halves(w1_raw[1]), "w1_1"))
-            if s in (1, 2):
-                raw = load_weight(w3, s - 1, 0, HALF, "page%d" % (s + 3))
-                w3_q[(s - 1, 0)] = quantise_weight(both_halves(raw), "w3_%d0" % (s - 1))
+            if s < 4:
+                g, a = s % 2, s // 2
+                raw = load_weight(w3, g, a * HALF, HALF, "page%d" % (s + 4))
+                w3_q[(g, a)] = quantise_weight(both_halves(raw), "w3_%d%d" % (g, a))
             if s == 4:
                 wgo_t = keep.tile([P, PACK, NP], F32, name="wgo_t", tag="table", align_bytes=64)
-                load_dealt(wgo_t, wgo, 0, PACK)
-            if s >= PACK:
-                i = s - PACK
-                w3_late.append(load_weight(w3, i // 2, HALF + (i % 2) * HALF // 2, HALF // 2, "wgs%d" % i))
+                load_dealt(wgo_t, wgo, 0, PACK, (0, 2, 1, 3))
         for hf in range(2):
-            x_q[(0, hf)] = quantise_x(x[0][hf], "xq0%d" % hf, "xq0%d" % hf, "st_d")
+            x_q[(0, hf)] = quantise_x(x[0][hf], "xq0%d" % hf, "xq0%d" % hf)
         x_q[(1, 0)] = quantise_x(x[1][0], "xq10", "xq10")
         for s in range(FIRST_DEFERRED, SLICES):
-            loads[(s, 1)] = load_half(load, s, 1, "load_t")
             prepare(s, 1, pick(s, 1))
 
         order = []
@@ -383,5 +388,3 @@ def tile_list_electrode_heat_page_kernel(
                 y_put(i - 2)
             if i == 2:
                 x_q[(1, 1)] = quantise_x(x[1][1], "xq11", "xq11")
-                for g in range(2):
-                    w3_q[(g, 1)] = quantise_weight([w3_late[2 * g][:], w3_late[2 * g + 1][:]], "w3_%d1" % g, "st_d")

@@ -25,8 +25,8 @@ SLICES = H // P
 LIST_HALF = HALF // 16
 FIRST_DEFERRED = 4
 LAG = 4
-DIRECT_EVERY = 4
-DIRECT_EVERY_Y = 4
+DIRECT_EVERY_Y = 16
+ROW_SLOTS = 7
 
 
 def tile_list_electrode_heat_page_kernel(
@@ -66,27 +66,27 @@ def tile_list_electrode_heat_page_kernel(
             return tile
 
         def load_scale_rows(queue, tile, dram):
-            for q in range(4):
-                queue.dma_start(tile[32 * q : 32 * q + 4, :].bitcast(I32), dram[0, 4 * q : 4 * q + 4, :].bitcast(I32))
+            for r in range(4):
+                queue.dma_start(tile[r:P:32, :].bitcast(I32), dram[0, r:16:4, :].bitcast(I32))
 
-        def load_dealt(tile, dram, t0, t1, quadrants):
+        def load_dealt(tile, dram, t0, t1, quadrants, columns=slice(0, S)):
             by_row = dram.rearrange("(q t) j -> q t j", t=PACK)
             for c in quadrants:
-                nc.sync.dma_start(tile[32 * c : 32 * (c + 1), :, :], by_row[:, t0:t1, :])
+                nc.sync.dma_start(tile[32 * c : 32 * (c + 1), :, columns], by_row[:, t0:t1, columns])
 
-        w2_s_raw = keep.tile([P, H], U8, name="w2_s_raw", align_bytes=64)
-        nc.vector.memset(w2_s_raw[:].bitcast(I32), 0)
-        tab_s = keep.tile([P, T], U8, name="tab_s", align_bytes=64)
+        tab_s = keep.tile([P, T], U8, name="tab_s", tag="spare0", align_bytes=64)
         nc.vector.memset(tab_s[:].bitcast(I32), 0)
+        w2_s_raw = keep.tile([P, H], U8, name="w2_s_raw", tag="w3_11", align_bytes=64)
+        nc.vector.memset(w2_s_raw[:].bitcast(I32), 0)
 
         idx = load_list(offs, "idx")
-        w2_w_raw = keep.tile([P, 2 * H], U8, name="w2_w_raw", align_bytes=64)
+        load_scale_rows(nc.sync, tab_s, tab_scales)
+        w2_w_raw = keep.tile([P, 2 * H], U8, name="w2_w_raw", tag="spare1", align_bytes=64)
         nc.sync.dma_start(w2_w_raw[:].bitcast(I32), w2_words[0].bitcast(I32))
         idx2 = load_list(offs2, "idx2")
-        load_scale_rows(nc.sync, w2_s_raw, w2_scales)
         tab_w = keep.tile([P, T], U32, name="tab_w", tag="table", align_bytes=64)
         nc.sync.dma_start(tab_w[:].bitcast(I32), tab_words[0].rearrange("p t i -> p (t i)").bitcast(I32))
-        load_scale_rows(nc.sync, tab_s, tab_scales)
+        load_scale_rows(nc.sync, w2_s_raw, w2_scales)
 
         def load_weight(dram, g, c0, width, slot):
             raw = keep.tile([P, PACK, width], F32, name="raw", tag=slot)
@@ -110,12 +110,15 @@ def tile_list_electrode_heat_page_kernel(
         def both_halves(raw):
             return [raw[:, :, 0 : HALF // 2], raw[:, :, HALF // 2 : HALF]]
 
-        def quantise_x(x_tile, name, tag, stage="grouped"):
-            grouped = ring.tile([P, PACK * HALF], BF16, name="grouped", tag=stage, align_bytes=64)
-            nc.scalar.copy(
-                grouped[:].rearrange("p (c i t) -> p c t i", i=4, t=PACK),
-                x_tile[:].rearrange("p t (c i) -> p c t i", i=4),
-            )
+        def quantise_x(x_tile, name, tag, pieces=1, spare=None):
+            if spare is None:
+                grouped = ring.tile([P, PACK * HALF], BF16, name="grouped", tag="grouped", align_bytes=64)
+            else:
+                grouped = keep.tile([P, PACK * HALF], BF16, name="grouped", tag=spare, align_bytes=64)
+            dst = grouped[:].rearrange("p (c i t) -> p c t i", i=4, t=PACK)
+            src = x_tile[:].rearrange("p t (c i) -> p c t i", i=4)
+            for c0 in range(0, P, P // pieces):
+                nc.scalar.copy(dst[:, c0 : c0 + P // pieces], src[:, c0 : c0 + P // pieces])
             return quantise(grouped, name, tag)
 
         def load_page(s):
@@ -123,8 +126,8 @@ def tile_list_electrode_heat_page_kernel(
             nc.sync.dma_start(tile[:], rows(page0, s))
             return tile
 
-        def load_rows(dram, s, name, bufs):
-            tile = ring.tile([P, S], F32, name=name, bufs=bufs)
+        def load_rows(dram, s, slot):
+            tile = keep.tile([P, S], F32, name="rows", tag="rows%d" % (slot % ROW_SLOTS))
             nc.sync.dma_start(tile[:], rows(dram, s))
             return tile
 
@@ -134,18 +137,20 @@ def tile_list_electrode_heat_page_kernel(
         wgs_t = [wgs_first[:, 0, :], wgs_second[:, 0, :], wgs_rest[:, 0, :], wgs_rest[:, 1, :]]
 
         w1_raw = [load_weight(w1, 0, 0, HALF, "page2")]
-        shifts = {0: load_rows(shift, 0, "shift_t", 3)}
-        load_dealt(wgs_first, wgs, 0, 1, (0, 2))
+        shifts = {0: load_rows(shift, 0, 0)}
+        load_dealt(wgs_first, wgs, 0, 1, (0, 2), cols(0))
         pages = [load_page(0)]
-        load_dealt(wgs_first, wgs, 0, 1, (1, 3))
-        shifts[1] = load_rows(shift, 1, "shift_t", 3)
-        loads = {0: load_rows(load, 0, "load_t", 4)}
+        load_dealt(wgs_first, wgs, 0, 1, (1, 3), cols(0))
+        load_dealt(wgs_first, wgs, 0, 1, (0, 2), cols(1))
+        shifts[1] = load_rows(shift, 1, 1)
+        load_dealt(wgs_first, wgs, 0, 1, (1, 3), cols(1))
         idx3 = load_list(offs3, "idx3")
+        shifts[2] = load_rows(shift, 2, 2)
         lim_t = load_vector(lim, "lim_t")
+        loads = {0: load_rows(load, 0, ROW_SLOTS - 1)}
         load_dealt(wgs_second, wgs, 1, 2, (0, 2))
         pages.append(load_page(1))
         load_dealt(wgs_second, wgs, 1, 2, (1, 3))
-        shifts[2] = load_rows(shift, 2, "shift_t", 3)
         w1_raw.append(load_weight(w1, 0, HALF, HALF, "page3"))
         load_dealt(wgs_rest, wgs, 2, 4, (0, 2, 1, 3))
         idx4 = load_list(offs4, "idx4")
@@ -157,15 +162,19 @@ def tile_list_electrode_heat_page_kernel(
         nc.scalar.activation(neg_base[:], base_t[:], ACT.Copy, scale=-1.0)
 
         w2_w = keep.tile([P, 2 * H], U8, name="w2_w", align_bytes=64)
-        nc.vector.tensor_copy(
-            w2_w[:].rearrange("p (a t m b) -> p a t m b", a=2, t=PACK, b=2),
-            w2_w_raw[:].rearrange("p (a m t b) -> p a t m b", a=2, t=PACK, b=2),
-        )
         w2_s = keep.tile([P, H], U8, name="w2_s", align_bytes=64)
-        nc.vector.tensor_copy(
-            w2_s[:].rearrange("p (a t m) -> p a t m", a=2, t=PACK),
-            w2_s_raw[:].rearrange("p (a m t) -> p a t m", a=2, t=PACK),
-        )
+
+        def deal_w2(a):
+            nc.vector.tensor_copy(
+                w2_w[:, 2 * a * HALF : 2 * (a + 1) * HALF].rearrange("p (t m b) -> p t m b", t=PACK, b=2),
+                w2_w_raw[:, 2 * a * HALF : 2 * (a + 1) * HALF].rearrange("p (m t b) -> p t m b", t=PACK, b=2),
+            )
+            nc.vector.tensor_copy(
+                w2_s[:, cols(a)].rearrange("p (t m) -> p t m", t=PACK),
+                w2_s_raw[:, cols(a)].rearrange("p (m t) -> p t m", t=PACK),
+            )
+
+        deal_w2(0)
         v_w, v_s = [], []
         for hf in range(2):
             words = keep.tile([P, HALF], U32, name="v_w%d" % hf, align_bytes=64)
@@ -186,6 +195,7 @@ def tile_list_electrode_heat_page_kernel(
                 in_=grouped[:, t0 * HALF : t1 * HALF],
             )
         w1_q = [(w1_codes, w1_scales)]
+        deal_w2(1)
 
         def bank(tag, bufs):
             return psum.tile([P, HALF], F32, name=tag, tag=tag, bufs=bufs)
@@ -201,38 +211,52 @@ def tile_list_electrode_heat_page_kernel(
         def staged(name):
             return ring.tile([P, HALF], F32, name=name, tag=name, align_bytes=64)
 
-        def first_products(s, hf, banks):
-            a, t = s // PACK, s % PACK
+        def product_w2(s, hf, banks):
             a2 = bank(banks, 2)
             nc.tensor.matmul_mx(
                 out=a2[:], lhsT=w2_w[:, 2 * s * P : 2 * (s + 1) * P].bitcast(FP4X4), lhsT_scale=w2_s[:, block(s)],
                 rhs=v_w[hf][:].bitcast(FP8X4), rhs_scale=v_s[hf][:], start=True, stop=True,
             )
+            return a2
+
+        def product_w1(s, hf, banks):
+            a, t = s // PACK, s % PACK
             a1 = bank(banks, 2)
             nc.tensor.matmul_mx(
                 out=a1[:], lhsT=w1_q[a][0][:, block(t)].bitcast(FP8X4), lhsT_scale=w1_q[a][1][:, block(t)],
                 rhs=v_w[hf][:].bitcast(FP8X4), rhs_scale=v_s[hf][:], start=True, stop=True,
             )
-            return a1, a2
+            return a1
 
         h_tiles = {}
         under_way = {}
 
         def on_vector(u):
-            return u < 2 or u % DIRECT_EVERY == 2
+            return u in (3, 5)
+
+        def first_h():
+            h_tiles[0] = ring.tile([P, S], F32, name="h", tag="result", bufs=3)
+            a2 = [product_w2(0, hf, "mx") for hf in range(2)]
+            a1 = [product_w1(0, hf, "direct") for hf in range(2)]
+            shifted = [staged("picked") for hf in range(2)]
+            for hf in range(2):
+                nc.vector.tensor_tensor(shifted[hf][:], a2[hf][:], shifts[0][:, cols(hf)], ALU.add)
+            for hf in range(2):
+                nc.vector.tensor_tensor(h_tiles[0][:, cols(hf)], a1[hf][:], shifted[hf][:], ALU.max)
 
         def h_products(u):
             s, hf = u // 2, u % 2
             if hf == 0:
                 h_tiles[s] = ring.tile([P, S], F32, name="h", tag="result", bufs=3)
             shift_t = shifts[s][:, cols(hf)]
+            banks = "direct" if on_vector(u) else "mx"
+            a2 = product_w2(s, hf, banks)
+            a1 = product_w1(s, hf, banks)
             if on_vector(u):
-                a1, a2 = first_products(s, hf, "mx" if u == 1 else "direct")
-                shifted = staged("picked")
+                shifted = keep.tile([P, HALF], F32, name="shifted", tag="spare1", align_bytes=64)
                 nc.vector.tensor_tensor(shifted[:], a2[:], shift_t, ALU.add)
                 nc.vector.tensor_tensor(h_tiles[s][:, cols(hf)], a1[:], shifted[:], ALU.max)
             else:
-                a1, a2 = first_products(s, hf, "mx")
                 a2_sb = staged("st_a")
                 nc.scalar.copy(a2_sb[:], a2[:])
                 neg_a1 = staged("st_b")
@@ -248,7 +272,10 @@ def tile_list_electrode_heat_page_kernel(
                 add_transposed(neg_a1_turned, [neg_a1])
                 relu_turned = staged("st_c")
                 nc.scalar.activation(relu_turned[:], excess[:], ACT.Relu)
-                a1_turned = staged("grouped" if u // 2 == SLICES - 2 else "st_d")
+                if u // 2 == SLICES - 2:
+                    a1_turned = keep.tile([P, HALF], F32, name="a1_turned", tag="spare%d" % (u % 2), align_bytes=64)
+                else:
+                    a1_turned = staged("st_d")
                 nc.scalar.activation(a1_turned[:], neg_a1_turned[:], ACT.Copy, scale=-1.0)
                 under_way[u] = (relu_turned, a1_turned)
 
@@ -280,16 +307,19 @@ def tile_list_electrode_heat_page_kernel(
         x_q = {}
         w3_q = {}
         wgo_t = None
-        for u in range(4):
-            h_step(u)
+        waiting = []
+        first_h()
+        h_step(2)
         for s in range(SLICES):
             halves = [0, 1] if s < FIRST_DEFERRED else [0]
             if 1 <= s < SLICES - 1:
                 pages.append(load_page(s + 1))
             if 1 <= s < SLICES - 2:
-                shifts[s + 2] = load_rows(shift, s + 2, "shift_t", 3)
-            if s + 1 < SLICES:
-                loads[s + 1] = load_rows(load, s + 1, "load_t", 4)
+                shifts[s + 2] = load_rows(shift, s + 2, s + 2)
+            for u in (2 * s + 3, 2 * s + 4):
+                h_step(u)
+            if s >= 2:
+                loads[s - 1] = load_rows(load, s - 1, s + 1)
 
             h = h_tiles.pop(s)
             weights = wgs_t[s % PACK]
@@ -300,12 +330,9 @@ def tile_list_electrode_heat_page_kernel(
                     )
             else:
                 nc.vector.tensor_tensor(pages[s][:].indirect(idx2[:]), h[:], weights, ALU.mult)
-            picked = [pick(s, hf) for hf in halves]
-            for hf in halves:
-                prepare(s, hf, picked[hf])
-            if s + 1 < SLICES:
-                for u in (2 * s + 4, 2 * s + 5):
-                    h_step(u)
+            for hf, picked in waiting:
+                prepare(s - 1, hf, picked)
+            waiting = [(hf, pick(s, hf)) for hf in halves]
 
             if s == 0:
                 w1_q.append(quantise_weight(both_halves(w1_raw[1]), "w1_1"))
@@ -316,8 +343,10 @@ def tile_list_electrode_heat_page_kernel(
             if s == 4:
                 wgo_t = keep.tile([P, PACK, NP], F32, name="wgo_t", tag="table", align_bytes=64)
                 load_dealt(wgo_t, wgo, 0, PACK, (0, 2, 1, 3))
+        loads[SLICES - 1] = load_rows(load, SLICES - 1, SLICES + 1)
+        prepare(SLICES - 1, 0, waiting[0][1])
         for hf in range(2):
-            x_q[(0, hf)] = quantise_x(x[0][hf], "xq0%d" % hf, "xq0%d" % hf)
+            x_q[(0, hf)] = quantise_x(x[0][hf], "xq0%d" % hf, "xq0%d" % hf, 2, "spare%d" % hf)
         x_q[(1, 0)] = quantise_x(x[1][0], "xq10", "xq10")
         for s in range(FIRST_DEFERRED, SLICES):
             prepare(s, 1, pick(s, 1))
@@ -387,4 +416,4 @@ def tile_list_electrode_heat_page_kernel(
             if i >= 2:
                 y_put(i - 2)
             if i == 2:
-                x_q[(1, 1)] = quantise_x(x[1][1], "xq11", "xq11")
+                x_q[(1, 1)] = quantise_x(x[1][1], "xq11", "xq11", 4)

from contextlib import ExitStack

import concourse.mybir as mybir
from concourse.masks import make_identity

K, H, T, S, T2, NP = 512, 1024, 4096, 1024, 2048, 1024
FLOPS = 2 * (2 * K * H * S + H * H * NP)

F32 = mybir.dt.float32
BF16 = mybir.dt.bfloat16
I32 = mybir.dt.int32
U32 = mybir.dt.uint32
U16 = mybir.dt.uint16
U8 = mybir.dt.uint8
FP8X4 = mybir.dt.float8_e4m3fn_x4
FP4X4 = mybir.dt.float4_e2m1fn_x4
ALU = mybir.AluOpType
ACT = mybir.ActivationFunctionType

P = 128
PACK = 4
HALF = 512
BLOCKS = HALF // P
SLICES = H // P
LIST_HALF = HALF // 16
FIRST_DEFERRED = 4
LAG = 4
DIRECT_EVERY_Y = 16
ROW_SLOTS = 7


def tile_list_electrode_heat_page_kernel(
    tc, tab_words, tab_scales, offs, offs2, offs3, offs4, w1, w2_words, w2_scales,
    shift, page0, wgs, lim, load, w3, base, wgo, out,
):
    nc = tc.nc

    def rows(dram, s):
        return dram.rearrange("(a p t) c -> a t p c", p=P, t=PACK)[s // PACK, s % PACK]

    def cols(hf):
        return slice(hf * HALF, (hf + 1) * HALF)

    def entries(hf):
        return slice(hf * LIST_HALF, (hf + 1) * LIST_HALF)

    def block(b):
        return slice(b * P, (b + 1) * P)

    with ExitStack() as ctx:
        lists = ctx.enter_context(tc.tile_pool(name="lists", bufs=1))
        keep = ctx.enter_context(tc.tile_pool(name="keep", bufs=1))
        ring = ctx.enter_context(tc.tile_pool(name="ring", bufs=2))
        psum = ctx.enter_context(tc.psum_pool(name="psum", bufs=1))

        def load_list(dram, name):
            tile = lists.tile([P, S // 16], U16, name=name)
            nc.sync.dma_start(tile[:], dram)
            return tile

        def load_vector(dram, name):
            tile = keep.tile([P, SLICES], F32, name=name)
            nc.sync.dma_start(
                tile[:].rearrange("p (a t) -> p a t", t=PACK), dram.rearrange("(a p t) -> p a t", p=P, t=PACK)
            )
            return tile

        def load_scale_rows(queue, tile, dram):
            for r in range(4):
                queue.dma_start(tile[r:P:32, :].bitcast(I32), dram[0, r:16:4, :].bitcast(I32))

        def load_dealt(tile, dram, t0, t1, quadrants, columns=slice(0, S)):
            by_row = dram.rearrange("(q t) j -> q t j", t=PACK)
            for c in quadrants:
                nc.sync.dma_start(tile[32 * c : 32 * (c + 1), :, columns], by_row[:, t0:t1, columns])

        tab_s = keep.tile([P, T], U8, name="tab_s", tag="spare0", align_bytes=64)
        nc.vector.memset(tab_s[:].bitcast(I32), 0)
        w2_s_raw = keep.tile([P, H], U8, name="w2_s_raw", tag="w3_11", align_bytes=64)
        nc.vector.memset(w2_s_raw[:].bitcast(I32), 0)

        idx = load_list(offs, "idx")
        load_scale_rows(nc.sync, tab_s, tab_scales)
        w2_w_raw = keep.tile([P, 2 * H], U8, name="w2_w_raw", tag="spare1", align_bytes=64)
        nc.sync.dma_start(w2_w_raw[:].bitcast(I32), w2_words[0].bitcast(I32))
        idx2 = load_list(offs2, "idx2")
        tab_w = keep.tile([P, T], U32, name="tab_w", tag="table", align_bytes=64)
        nc.sync.dma_start(tab_w[:].bitcast(I32), tab_words[0].rearrange("p t i -> p (t i)").bitcast(I32))
        load_scale_rows(nc.sync, w2_s_raw, w2_scales)

        def load_weight(dram, g, c0, width, slot):
            raw = keep.tile([P, PACK, width], F32, name="raw", tag=slot)
            k_rows = dram[g * P * PACK : (g + 1) * P * PACK, c0 : c0 + width]
            nc.sync.dma_start(raw[:], k_rows.rearrange("(p j) c -> p j c", j=PACK))
            return raw

        def quantise(grouped, name, tag):
            codes = keep.tile([P, HALF], U32, name=name + "_c", tag=tag, align_bytes=64)
            scales = keep.tile([P, HALF], U8, name=name + "_s", align_bytes=64)
            nc.vector.quantize_mx(out=codes[:].bitcast(FP8X4), scales=scales[:], in_=grouped[:])
            return codes, scales

        def quantise_weight(pieces, name, stage="grouped"):
            grouped = ring.tile([P, PACK * HALF], BF16, name="grouped", tag=stage, align_bytes=64)
            dst = grouped[:].rearrange("p (t m j) -> p m j t", t=PACK, j=PACK)
            for i, piece in enumerate(pieces):
                nc.scalar.copy(dst[:, i * P // 2 : (i + 1) * P // 2], piece.rearrange("p j (m t) -> p m j t", t=PACK))
            return quantise(grouped, name, name)

        def both_halves(raw):
            return [raw[:, :, 0 : HALF // 2], raw[:, :, HALF // 2 : HALF]]

        def quantise_x(x_tile, name, tag, pieces=1, spare=None):
            if spare is None:
                grouped = ring.tile([P, PACK * HALF], BF16, name="grouped", tag="grouped", align_bytes=64)
            else:
                grouped = keep.tile([P, PACK * HALF], BF16, name="grouped", tag=spare, align_bytes=64)
            dst = grouped[:].rearrange("p (c i t) -> p c t i", i=4, t=PACK)
            src = x_tile[:].rearrange("p t (c i) -> p c t i", i=4)
            for c0 in range(0, P, P // pieces):
                nc.scalar.copy(dst[:, c0 : c0 + P // pieces], src[:, c0 : c0 + P // pieces])
            return quantise(grouped, name, tag)

        def load_page(s):
            tile = keep.tile([P, T2], F32, name="page", tag="page%d" % s)
            nc.sync.dma_start(tile[:], rows(page0, s))
            return tile

        def load_rows(dram, s, slot):
            tile = keep.tile([P, S], F32, name="rows", tag="rows%d" % (slot % ROW_SLOTS))
            nc.sync.dma_start(tile[:], rows(dram, s))
            return tile

        wgs_first = keep.tile([P, 1, S], F32, name="wgs_first")
        wgs_second = keep.tile([P, 1, S], F32, name="wgs_second")
        wgs_rest = keep.tile([P, 2, S], F32, name="wgs_rest")
        wgs_t = [wgs_first[:, 0, :], wgs_second[:, 0, :], wgs_rest[:, 0, :], wgs_rest[:, 1, :]]

        w1_raw = [load_weight(w1, 0, 0, HALF, "page2")]
        shifts = {0: load_rows(shift, 0, 0)}
        load_dealt(wgs_first, wgs, 0, 1, (0, 2), cols(0))
        pages = [load_page(0)]
        load_dealt(wgs_first, wgs, 0, 1, (1, 3), cols(0))
        load_dealt(wgs_first, wgs, 0, 1, (0, 2), cols(1))
        shifts[1] = load_rows(shift, 1, 1)
        load_dealt(wgs_first, wgs, 0, 1, (1, 3), cols(1))
        idx3 = load_list(offs3, "idx3")
        shifts[2] = load_rows(shift, 2, 2)
        lim_t = load_vector(lim, "lim_t")
        loads = {0: load_rows(load, 0, ROW_SLOTS - 1)}
        load_dealt(wgs_second, wgs, 1, 2, (0, 2))
        pages.append(load_page(1))
        load_dealt(wgs_second, wgs, 1, 2, (1, 3))
        w1_raw.append(load_weight(w1, 0, HALF, HALF, "page3"))
        load_dealt(wgs_rest, wgs, 2, 4, (0, 2, 1, 3))
        idx4 = load_list(offs4, "idx4")
        base_t = load_vector(base, "base_t")

        ident = keep.tile([P, P], F32, name="ident")
        make_identity(nc, ident[:])
        neg_base = keep.tile([P, SLICES], F32, name="neg_base")
        nc.scalar.activation(neg_base[:], base_t[:], ACT.Copy, scale=-1.0)

        w2_w = keep.tile([P, 2 * H], U8, name="w2_w", align_bytes=64)
        w2_s = keep.tile([P, H], U8, name="w2_s", align_bytes=64)

        def deal_w2(a):
            nc.vector.tensor_copy(
                w2_w[:, 2 * a * HALF : 2 * (a + 1) * HALF].rearrange("p (t m b) -> p t m b", t=PACK, b=2),
                w2_w_raw[:, 2 * a * HALF : 2 * (a + 1) * HALF].rearrange("p (m t b) -> p t m b", t=PACK, b=2),
            )
            nc.vector.tensor_copy(
                w2_s[:, cols(a)].rearrange("p (t m) -> p t m", t=PACK),
                w2_s_raw[:, cols(a)].rearrange("p (m t) -> p t m", t=PACK),
            )

        deal_w2(0)
        v_w, v_s = [], []
        for hf in range(2):
            words = keep.tile([P, HALF], U32, name="v_w%d" % hf, align_bytes=64)
            nc.vector.tensor_copy(words[:], tab_w[:].indirect(idx[:, entries(hf)]))
            scale_bytes = keep.tile([P, HALF], U8, name="v_s%d" % hf, align_bytes=64)
            nc.vector.tensor_copy(scale_bytes[:], tab_s[:].indirect(idx[:, entries(hf)]))
            v_w.append(words)
            v_s.append(scale_bytes)
        grouped = ring.tile([P, PACK * HALF], BF16, name="grouped", tag="grouped", align_bytes=64)
        w1_codes = keep.tile([P, HALF], U32, name="w1_0_c", align_bytes=64)
        w1_scales = keep.tile([P, HALF], U8, name="w1_0_s", align_bytes=64)
        dst = grouped[:].rearrange("p (t m j) -> p m j t", t=PACK, j=PACK)
        src = w1_raw[0][:].rearrange("p j (m t) -> p m j t", t=PACK)
        for t0, t1 in ((0, 1), (1, PACK)):
            nc.scalar.copy(dst[:, :, :, t0:t1], src[:, :, :, t0:t1])
            nc.vector.quantize_mx(
                out=w1_codes[:, t0 * P : t1 * P].bitcast(FP8X4), scales=w1_scales[:, t0 * P : t1 * P],
                in_=grouped[:, t0 * HALF : t1 * HALF],
            )
        w1_q = [(w1_codes, w1_scales)]
        deal_w2(1)

        def bank(tag, bufs):
            return psum.tile([P, HALF], F32, name=tag, tag=tag, bufs=bufs)

        def add_transposed(dst, terms):
            for b in range(BLOCKS):
                for i, term in enumerate(terms):
                    nc.tensor.matmul(
                        dst[:, block(b)], term[:, block(b)], ident[:],
                        start=(i == 0), stop=(i == len(terms) - 1), is_transpose=True,
                    )

        def staged(name):
            return ring.tile([P, HALF], F32, name=name, tag=name, align_bytes=64)

        def product_w2(s, hf, banks):
            a2 = bank(banks, 2)
            nc.tensor.matmul_mx(
                out=a2[:], lhsT=w2_w[:, 2 * s * P : 2 * (s + 1) * P].bitcast(FP4X4), lhsT_scale=w2_s[:, block(s)],
                rhs=v_w[hf][:].bitcast(FP8X4), rhs_scale=v_s[hf][:], start=True, stop=True,
            )
            return a2

        def product_w1(s, hf, banks):
            a, t = s // PACK, s % PACK
            a1 = bank(banks, 2)
            nc.tensor.matmul_mx(
                out=a1[:], lhsT=w1_q[a][0][:, block(t)].bitcast(FP8X4), lhsT_scale=w1_q[a][1][:, block(t)],
                rhs=v_w[hf][:].bitcast(FP8X4), rhs_scale=v_s[hf][:], start=True, stop=True,
            )
            return a1

        h_tiles = {}
        under_way = {}

        def on_vector(u):
            return u in (3, 5)

        def first_h():
            h_tiles[0] = ring.tile([P, S], F32, name="h", tag="result", bufs=3)
            a2 = [product_w2(0, hf, "mx") for hf in range(2)]
            a1 = [product_w1(0, hf, "direct") for hf in range(2)]
            shifted = [staged("picked") for hf in range(2)]
            for hf in range(2):
                nc.vector.tensor_tensor(shifted[hf][:], a2[hf][:], shifts[0][:, cols(hf)], ALU.add)
            for hf in range(2):
                nc.vector.tensor_tensor(h_tiles[0][:, cols(hf)], a1[hf][:], shifted[hf][:], ALU.max)

        def h_products(u):
            s, hf = u // 2, u % 2
            if hf == 0:
                h_tiles[s] = ring.tile([P, S], F32, name="h", tag="result", bufs=3)
            shift_t = shifts[s][:, cols(hf)]
            banks = "direct" if on_vector(u) else "mx"
            a2 = product_w2(s, hf, banks)
            a1 = product_w1(s, hf, banks)
            if on_vector(u):
                shifted = keep.tile([P, HALF], F32, name="shifted", tag="spare1", align_bytes=64)
                nc.vector.tensor_tensor(shifted[:], a2[:], shift_t, ALU.add)
                nc.vector.tensor_tensor(h_tiles[s][:, cols(hf)], a1[:], shifted[:], ALU.max)
            else:
                a2_sb = staged("st_a")
                nc.scalar.copy(a2_sb[:], a2[:])
                neg_a1 = staged("st_b")
                nc.scalar.activation(neg_a1[:], a1[:], ACT.Copy, scale=-1.0)
                under_way[u] = (shift_t, a2_sb, neg_a1)

        def h_excess(u):
            if u in under_way:
                shift_t, a2_sb, neg_a1 = under_way[u]
                excess = bank("turned", 2)
                add_transposed(excess, [shift_t, a2_sb, neg_a1])
                neg_a1_turned = bank("turned", 2)
                add_transposed(neg_a1_turned, [neg_a1])
                relu_turned = staged("st_c")
                nc.scalar.activation(relu_turned[:], excess[:], ACT.Relu)
                if u // 2 == SLICES - 2:
                    a1_turned = keep.tile([P, HALF], F32, name="a1_turned", tag="spare%d" % (u % 2), align_bytes=64)
                else:
                    a1_turned = staged("st_d")
                nc.scalar.activation(a1_turned[:], neg_a1_turned[:], ACT.Copy, scale=-1.0)
                under_way[u] = (relu_turned, a1_turned)

        def h_finish(u):
            if u in under_way:
                total = bank("back", 2)
                add_transposed(total, under_way.pop(u))
                nc.scalar.copy(h_tiles[u // 2][:, cols(u % 2)], total[:])

        def h_step(u):
            if u < 2 * SLICES:
                h_products(u)
            h_excess(u - 1)
            h_finish(u - 2)

        x = [[keep.tile([P, PACK, HALF], F32, name="x%d%d" % (a, hf)) for hf in range(2)] for a in range(2)]

        def pick(s, hf):
            picked = staged("picked")
            nc.vector.tensor_copy(picked[:], pages[s][:].indirect(idx3[:, entries(hf)]))
            return picked

        def prepare(s, hf, picked):
            nc.vector.scalar_tensor_tensor(
                out=x[s // PACK][hf][:, s % PACK, :], in0=picked[:], scalar=lim_t[:, s : s + 1],
                in1=loads[s][:, cols(hf)], op0=ALU.max, op1=ALU.mult,
            )

        x_q = {}
        w3_q = {}
        wgo_t = None
        waiting = []
        first_h()
        h_step(2)
        for s in range(SLICES):
            halves = [0, 1] if s < FIRST_DEFERRED else [0]
            if 1 <= s < SLICES - 1:
                pages.append(load_page(s + 1))
            if 1 <= s < SLICES - 2:
                shifts[s + 2] = load_rows(shift, s + 2, s + 2)
            for u in (2 * s + 3, 2 * s + 4):
                h_step(u)
            if s >= 2:
                loads[s - 1] = load_rows(load, s - 1, s + 1)

            h = h_tiles.pop(s)
            weights = wgs_t[s % PACK]
            if s == 0:
                for hf in range(2):
                    nc.vector.tensor_tensor(
                        pages[s][:].indirect(idx2[:, entries(hf)]), h[:, cols(hf)], weights[:, cols(hf)], ALU.mult
                    )
            else:
                nc.vector.tensor_tensor(pages[s][:].indirect(idx2[:]), h[:], weights, ALU.mult)
            for hf, picked in waiting:
                prepare(s - 1, hf, picked)
            waiting = [(hf, pick(s, hf)) for hf in halves]

            if s == 0:
                w1_q.append(quantise_weight(both_halves(w1_raw[1]), "w1_1"))
            if s < 4:
                g, a = s % 2, s // 2
                raw = load_weight(w3, g, a * HALF, HALF, "page%d" % (s + 4))
                w3_q[(g, a)] = quantise_weight(both_halves(raw), "w3_%d%d" % (g, a))
            if s == 4:
                wgo_t = keep.tile([P, PACK, NP], F32, name="wgo_t", tag="table", align_bytes=64)
                load_dealt(wgo_t, wgo, 0, PACK, (0, 2, 1, 3))
        loads[SLICES - 1] = load_rows(load, SLICES - 1, SLICES + 1)
        prepare(SLICES - 1, 0, waiting[0][1])
        for hf in range(2):
            x_q[(0, hf)] = quantise_x(x[0][hf], "xq0%d" % hf, "xq0%d" % hf, 2, "spare%d" % hf)
        x_q[(1, 0)] = quantise_x(x[1][0], "xq10", "xq10")
        for s in range(FIRST_DEFERRED, SLICES):
            prepare(s, 1, pick(s, 1))

        order = []
        for step in range(SLICES + LAG):
            if step < SLICES:
                order.append((step, 0))
            if step >= LAG:
                order.append((step - LAG, 1))
        scored = {}

        def y_product(i):
            s, hf = order[i]
            a, t = s // PACK, s % PACK
            direct = i % DIRECT_EVERY_Y == 0
            d = bank("direct" if direct else "mx", 2)
            for g in range(2):
                nc.tensor.matmul_mx(
                    out=d[:], lhsT=w3_q[(g, a)][0][:, block(t)].bitcast(FP8X4), lhsT_scale=w3_q[(g, a)][1][:, block(t)],
                    rhs=x_q[(g, hf)][0][:].bitcast(FP8X4), rhs_scale=x_q[(g, hf)][1][:], start=(g == 0), stop=(g == 1),
                )
            if direct:
                scored[i] = (True, d)
            else:
                above = staged("st_a")
                nc.scalar.activation(above[:], d[:], ACT.Relu, bias=neg_base[:, s : s + 1])
                scored[i] = (False, above)

        def y_sum(i):
            s, hf = order[i]
            direct, above = scored[i]
            if not direct:
                turned = bank("turned", 2)
                add_transposed(turned, [x[s // PACK][hf][:, s % PACK, :], above])
                turned_sb = staged("st_c")
                nc.scalar.copy(turned_sb[:], turned[:])
                scored[i] = (False, turned_sb)

        def y_put(i):
            s, hf = order[i]
            direct, source = scored.pop(i)
            if i == 0:
                y = keep.tile([P, HALF], F32, name="y_first", tag="xq11", align_bytes=64)
            else:
                y = ring.tile([P, HALF], F32, name="y", tag="result", bufs=3)
            if direct:
                nc.vector.scalar_tensor_tensor(
                    out=y[:], in0=source[:], scalar=base_t[:, s : s + 1], in1=x[s // PACK][hf][:, s % PACK, :],
                    op0=ALU.max, op1=ALU.add,
                )
            else:
                total = bank("back", 2)
                add_transposed(total, [source])
                nc.scalar.activation(y[:], total[:], ACT.Identity, bias=base_t[:, s : s + 1])
            nc.vector.tensor_tensor(
                pages[s][:].indirect(idx4[:, entries(hf)]), y[:], wgo_t[:, s % PACK, cols(hf)], ALU.mult
            )
            if hf == 1:
                nc.sync.dma_start(rows(out, s), pages[s][:])

        for i in range(len(order) + 2):
            if i < len(order):
                y_product(i)
            if 1 <= i <= len(order):
                y_sum(i - 1)
            if i >= 2:
                y_put(i - 2)
            if i == 2:
                x_q[(1, 1)] = quantise_x(x[1][1], "xq11", "xq11", 4)
